import numpy as np
import ml_dtypes


def mxq(x, axis, fmt="e4m3"):
    dtype, down = {"e4m3": (ml_dtypes.float8_e4m3fn, 7), "e5m2": (ml_dtypes.float8_e5m2, 14)}[fmt]
    v = np.moveaxis(np.asarray(x, np.float32).astype(ml_dtypes.bfloat16).astype(np.float64), axis, -1)
    blocks = v.reshape(v.shape[:-1] + (-1, 32))
    amax = np.abs(blocks).max(-1, keepdims=True)
    byte = np.maximum(np.where(amax > 0, np.frexp(amax)[1] - 1 + 127, 0) - down, 1)
    scale = np.exp2(byte - 127.0)
    codes = (blocks / scale).astype(np.float32).astype(dtype).astype(np.float64)
    return np.moveaxis((codes * scale).reshape(v.shape), -1, axis)


WIDE = False


def mx_kscale(k):
    if not WIDE:
        return np.ones(k)
    levels = np.array([10, -10, 5, -5, 0])
    if k % 512:
        return np.exp2(np.random.permutation(np.resize(levels, k // 32))).repeat(32)
    a = np.empty((k // 512, 16))
    for p in range(k // 512):
        a[p, :8] = np.random.permutation(np.resize(levels, 8))
        for g in range(8):
            far = levels[np.abs(levels - a[p, g]) >= 10]
            a[p, g + 8] = far[np.random.randint(len(far))]
    return np.exp2(a.ravel()).repeat(32)


def f64(x):
    return np.asarray(x).astype(np.float64)


def striped(idx):
    return np.tile(idx.reshape(-1, 16).T, (8, 1)).astype(np.uint16)


def unstriped(offs):
    return offs[:16].T.reshape(-1).astype(np.int64)


E2M1 = np.array([0.0, 0.5, 1.0, 1.5, 2.0, 3.0, 4.0, 6.0, -0.0, -0.5, -1.0, -1.5, -2.0, -3.0, -4.0, -6.0])


def pack_weight(w, fmt):
    k, n = w.shape
    w = f64(np.asarray(w, np.float32).astype(ml_dtypes.bfloat16)).reshape(k // 32, 32, n)
    amax = np.abs(w).max(1)
    if fmt == "e4m3":
        byte = np.frexp(amax)[1] - 1 + 127 - 7
    else:
        mant, ex = np.frexp(amax / 6.0)
        byte = np.where(mant > 0.5, ex, ex - 1) + 127
    byte = np.clip(np.where(amax > 0, byte, 1), 1, 254)
    scaled = (w * np.exp2(127.0 - byte)[:, None, :]).reshape(k, n).astype(np.float32)
    by_word = np.ascontiguousarray(scaled.reshape(k // 512, 128, 4, n).transpose(0, 1, 3, 2))
    if fmt == "e4m3":
        words = by_word.astype(ml_dtypes.float8_e4m3fn).view(np.uint8)
    else:
        c = by_word.astype(ml_dtypes.float4_e2m1fn).view(np.uint8) & 0xF
        words = (c[..., 0::2] | (c[..., 1::2] << 4)).reshape(k // 512, 128, 2 * n)
    return np.ascontiguousarray(words), np.ascontiguousarray(byte.astype(np.uint8).reshape(k // 512, 16, n))


def unpack_weight(words, scales, fmt):
    g, _, n = scales.shape
    words = np.ascontiguousarray(words).reshape(g, 128, n, -1)
    if fmt == "e4m3":
        vals = words.view(ml_dtypes.float8_e4m3fn).astype(np.float64)
    else:
        nib = np.empty((g, 128, n, 4), np.uint8)
        nib[..., 0::2] = words & 0xF
        nib[..., 1::2] = words >> 4
        vals = E2M1[nib]
    vals = vals * np.repeat(np.exp2(scales.astype(np.float64) - 127.0), 8, axis=1)[..., None]
    return vals.transpose(0, 1, 3, 2).reshape(g * 512, n)


def gelu(v):
    return 0.5 * v * (1.0 + np.tanh(np.sqrt(2.0 / np.pi) * (v + 0.044715 * v**3)))


K, H, N, T, S, P1, P2, P3 = 1024, 512, 512, 4096, 2048, 1024, 512, 256

def setup_inputs():
    n = np.random.standard_normal
    s = mx_kscale(K)[:, None]
    u = mx_kscale(H)[:, None]
    tab_words, tab_scales = pack_weight(n((K, T)) * s, "e4m3")
    w1 = 0.52 * n((K, H)) / np.sqrt(K) / s
    gain = np.exp(0.4 * n(H)) * u[:, 0]
    w4_words, w4_scales = pack_weight(2.2 * n((H, N)) / np.sqrt(H) / u, "e2m1")
    return {
        "tab_words": tab_words, "tab_scales": tab_scales,
        "offs": striped(np.random.permutation(T)[:S]),
        "pos1": striped(np.random.permutation(S)[:P1]),
        "pos2": striped(np.random.permutation(S)[:P1]),
        "pos3": striped(np.random.permutation(P1)[:P2]),
        "pos4": striped(np.random.permutation(P1)[:P2]),
        "pos5": striped(np.random.permutation(P2)[:P3]),
        "pos6": striped(np.random.permutation(P2)[:P3]),
        "w1": w1.astype(np.float32),
        "gain": gain.astype(np.float32),
        "w4_words": w4_words, "w4_scales": w4_scales,
    }

def reference(tab_words, tab_scales, offs, pos1, pos2, pos3, pos4, pos5, pos6, w1, gain, w4_words, w4_scales):
    v = unpack_weight(tab_words, tab_scales, "e4m3")[:, unstriped(offs)]
    h = np.sin(mxq(f64(w1), 0, "e4m3").T @ v)
    left = h[:, unstriped(pos1)]
    right = h[:, unstriped(pos2)]
    a1 = (left * right + left) * f64(gain)[:, None]
    a2 = np.minimum(a1[:, unstriped(pos3)], a1[:, unstriped(pos4)])
    a3 = a2[:, unstriped(pos5)] + a2[:, unstriped(pos6)]
    w4 = unpack_weight(w4_words, w4_scales, "e2m1")
    y = w4.T @ mxq(a3, 0, "e4m3")
    return 1.0 / (1.0 + np.exp(-y))

@@ -1,0 +1,218 @@
+import math
+from contextlib import ExitStack
+
+import concourse.mybir as mybir
+from concourse.masks import make_identity
+
+K, H, N, T, S = 1024, 512, 512, 4096, 2048
+P1, P2, P3 = 1024, 512, 256
+FLOPS = 2 * K * H * S + 2 * H * N * P3
+
+F32 = mybir.dt.float32
+BF16 = mybir.dt.bfloat16
+I32 = mybir.dt.int32
+U32 = mybir.dt.uint32
+U16 = mybir.dt.uint16
+U8 = mybir.dt.uint8
+FP8X4 = mybir.dt.float8_e4m3fn_x4
+FP4X4 = mybir.dt.float4_e2m1fn_x4
+ALU = mybir.AluOpType
+ACT = mybir.ActivationFunctionType
+
+P = 128
+PACK = 4
+PASSES = K // (P * PACK)
+CHUNK = 512
+CHUNKS = S // CHUNK
+BLOCKS = CHUNK // P
+LIST_ROWS = 16
+
+TURN_BASE = 98304.0
+TURN_BASE_BITS = float(0x47C00000)
+BITS_PER_TURN = 128.0
+
+
+def tile_list_panel_programme_features_kernel(
+    tc, tab_words, tab_scales, offs, pos1, pos2, pos3, pos4, pos5, pos6, w1, gain, w4_words, w4_scales, out
+):
+    nc = tc.nc
+    with ExitStack() as ctx:
+        lists = ctx.enter_context(tc.tile_pool(name="lists", bufs=1))
+        keep = ctx.enter_context(tc.tile_pool(name="keep", bufs=1))
+        ring = ctx.enter_context(tc.tile_pool(name="ring", bufs=3))
+        pair = ctx.enter_context(tc.tile_pool(name="pair", bufs=2))
+        sums = ctx.enter_context(tc.psum_pool(name="sums", bufs=4))
+        turned = ctx.enter_context(tc.psum_pool(name="turned", bufs=3))
+
+        def load_list(src, name):
+            held = lists.tile(list(src.shape), U16, name=name)
+            nc.sync.dma_start(held[:], src)
+            return held
+
+        def load_w1(a):
+            raw = keep.tile([P, PACK, H], F32, name="w1_raw%d" % a)
+            nc.sync.dma_start(raw[:], w1[a * P * PACK : (a + 1) * P * PACK, :].rearrange("(p j) r -> p j r", j=PACK))
+            return raw
+
+        def load_words(a):
+            words = keep.tile([P, T], I32, name="table_words%d" % a)
+            nc.sync.dma_start(words[:], tab_words[a].rearrange("p t i -> p (t i)").bitcast(I32))
+            return words
+
+        table_scales = keep.tile([P, T], U8, name="table_scales")
+        nc.vector.memset(table_scales[:].bitcast(I32), 0)
+        w4_plane = keep.tile([P, N], U8, name="w4_plane", align_bytes=64)
+        nc.vector.memset(w4_plane[:].bitcast(I32), 0)
+
+        idx = load_list(offs, "idx")
+        w1_raw = [load_w1(0)]
+        for q in range(4):
+            nc.sync.dma_start(
+                table_scales[32 * q : 32 * q + 4 * PASSES, :].bitcast(I32),
+                tab_scales[:, 4 * q : 4 * q + 4, :].bitcast(I32),
+            )
+        table_words = [load_words(0)]
+        w1_raw.append(load_w1(1))
+        table_words.append(load_words(1))
+        p2 = load_list(pos2, "p2")
+        p1 = load_list(pos1, "p1")
+        p3 = load_list(pos3, "p3")
+        p4 = load_list(pos4, "p4")
+        p5 = load_list(pos5, "p5")
+        p6 = load_list(pos6, "p6")
+        gains = keep.tile([P, PACK], F32, name="gains")
+        nc.sync.dma_start(gains[:], gain.rearrange("(p t) -> p t", t=PACK))
+        w4_codes = keep.tile([P, 2 * N], U8, name="w4_codes", align_bytes=64)
+        nc.sync.dma_start(w4_codes[:].bitcast(I32), w4_words[0].bitcast(I32))
+        for q in range(4):
+            nc.sync.dma_start(
+                w4_plane[32 * q : 32 * q + 4, :].bitcast(I32), w4_scales[0, 4 * q : 4 * q + 4, :].bitcast(I32)
+            )
+
+        identity = keep.tile([P, P], F32, name="identity")
+        make_identity(nc, identity[:])
+        minus_base = keep.tile([P, P], F32, name="minus_base")
+        nc.gpsimd.memset(minus_base[:], -TURN_BASE)
+
+        w1_codes, w1_planes = [], []
+
+        def quantise_w1(a):
+            grouped = keep.tile([P, H * PACK], BF16, name="w1_grouped%d" % a, align_bytes=64)
+            nc.scalar.copy(
+                grouped[:].rearrange("p (t m j) -> p m j t", t=PACK, j=PACK),
+                w1_raw[a][:].rearrange("p j (m t) -> p m j t", t=PACK),
+            )
+            codes = keep.tile([P, H], U32, name="w1_codes%d" % a, align_bytes=64)
+            plane = keep.tile([P, H], U8, name="w1_plane%d" % a, align_bytes=64)
+            nc.vector.quantize_mx(out=codes[:].bitcast(FP8X4), scales=plane[:], in_=grouped[:])
+            w1_codes.append(codes)
+            w1_planes.append(plane)
+
+        picked_scales = keep.tile([P, S], U8, name="picked_scales", align_bytes=64)
+        nc.vector.tensor_copy(picked_scales[:], table_scales[:].indirect(idx[:]))
+        quantise_w1(0)
+        picked0 = keep.tile([P, S], U32, name="picked_words0", align_bytes=64)
+        nc.vector.tensor_copy(picked0[:], table_words[0][:].bitcast(U32).indirect(idx[:]))
+        quantise_w1(1)
+        picked1 = keep.tile([P, S], U32, name="picked_words1", align_bytes=64)
+        cols = CHUNK // LIST_ROWS
+        for c in range(CHUNKS):
+            nc.vector.tensor_copy(
+                picked1[:, c * CHUNK : (c + 1) * CHUNK],
+                table_words[1][:].bitcast(U32).indirect(idx[:, c * cols : (c + 1) * cols]),
+            )
+        picked_words = [picked0, picked1]
+
+        h = [keep.tile([P, S], F32, name="h%d" % t) for t in range(PACK)]
+        a3 = keep.tile([P, PACK, P3], F32, name="a3")
+
+        def features(t, c):
+            x = sums.tile([P, CHUNK], F32, name="x", tag="sums")
+            rows = slice(t * P, (t + 1) * P)
+            for b in range(BLOCKS):
+                picks = slice(c * CHUNK + b * P, c * CHUNK + (b + 1) * P)
+                for a in range(PASSES):
+                    nc.tensor.matmul_mx(
+                        out=x[:, b * P : (b + 1) * P],
+                        lhsT=picked_words[a][:, picks].bitcast(FP8X4),
+                        lhsT_scale=picked_scales[4 * a :, picks],
+                        rhs=w1_codes[a][:, rows].bitcast(FP8X4),
+                        rhs_scale=w1_planes[a][:, rows],
+                        start=(a == 0),
+                        stop=(a == PASSES - 1),
+                    )
+            whole = ring.tile([P, CHUNK], U32, name="whole")
+            nc.scalar.activation(
+                whole[:], x[:], ACT.Copy, scale=-BITS_PER_TURN / (2.0 * math.pi), bias=TURN_BASE_BITS
+            )
+            turns = ring.tile([P, CHUNK], F32, name="turns")
+            nc.scalar.activation(turns[:], x[:], ACT.Copy, scale=1.0 / (2.0 * math.pi))
+            rest = turned.tile([P, CHUNK], F32, name="rest")
+            for b in range(BLOCKS):
+                blk = slice(b * P, (b + 1) * P)
+                terms = (minus_base[:], whole[:, blk].bitcast(F32), turns[:, blk])
+                for i, term in enumerate(terms):
+                    nc.tensor.matmul(
+                        rest[:, blk], term, identity[:], is_transpose=True, start=(i == 0), stop=(i == len(terms) - 1)
+                    )
+            nc.scalar.activation(h[t][:, c * CHUNK : (c + 1) * CHUNK], rest[:], ACT.Sin, scale=2.0 * math.pi)
+
+        def levels(t):
+            right = pair.tile([P, P1], F32, name="right")
+            half = P1 // 2
+            for s in range(2):
+                nc.vector.tensor_scalar(
+                    right[:, s * half : (s + 1) * half],
+                    h[t][:].indirect(p2[:, s * half // LIST_ROWS : (s + 1) * half // LIST_ROWS]),
+                    1.0,
+                    1.0,
+                    ALU.mult,
+                    ALU.add,
+                )
+            a1 = pair.tile([P, P1], F32, name="a1")
+            nc.vector.tensor_tensor(a1[:], h[t][:].indirect(p1[:]), right[:], ALU.mult)
+            first = pair.tile([P, P2], F32, name="first")
+            second = pair.tile([P, P2], F32, name="second")
+            nc.vector.tensor_copy(first[:], a1[:].indirect(p3[:]))
+            nc.vector.tensor_copy(second[:], a1[:].indirect(p4[:]))
+            a2 = pair.tile([P, P2], F32, name="a2")
+            nc.vector.tensor_tensor(a2[:], first[:], second[:], ALU.min)
+            term = pair.tile([P, P3], F32, name="term")
+            nc.vector.tensor_copy(term[:], a2[:].indirect(p5[:]))
+            nc.vector.tensor_tensor(a3[:, t, :], a2[:].indirect(p6[:]), term[:], ALU.add)
+
+        for t in range(PACK):
+            for c in range(CHUNKS):
+                features(t, c)
+            levels(t)
+
+        a3_grouped = keep.tile([P, P3, PACK], BF16, name="a3_grouped", align_bytes=64)
+        nc.vector.tensor_tensor(
+            a3_grouped[:],
+            a3[:].rearrange("p t j -> p j t"),
+            gains[:].unsqueeze(1).to_broadcast([P, P3, PACK]),
+            ALU.mult,
+        )
+        a3_codes = keep.tile([P, P3], U32, name="a3_codes", align_bytes=64)
+        a3_plane = keep.tile([P, P3], U8, name="a3_plane", align_bytes=64)
+        nc.vector.quantize_mx(
+            out=a3_codes[:].bitcast(FP8X4), scales=a3_plane[:], in_=a3_grouped[:].rearrange("p j t -> p (j t)")
+        )
+
+        out_rows = out.rearrange("(b p) j -> p b j", p=P)
+        for bank in range(2):
+            y = sums.tile([P, 2, P3], F32, name="y", tag="sums")
+            for i in range(2):
+                b = 2 * bank + i
+                nc.tensor.matmul_mx(
+                    out=y[:, i, :],
+                    lhsT=w4_codes[:, 2 * P * b : 2 * P * (b + 1)].bitcast(FP4X4),
+                    lhsT_scale=w4_plane[:, P * b : P * (b + 1)],
+                    rhs=a3_codes[:].bitcast(FP8X4),
+                    rhs_scale=a3_plane[:],
+                    start=True,
+                    stop=True,
+                )
+            scores = pair.tile([P, 2, P3], F32, name="scores")
+            nc.scalar.activation(scores[:], y[:], ACT.Sigmoid)
+            nc.sync.dma_start(out_rows[:, 2 * bank : 2 * bank + 2, :], scores[:])

@@ -39,10 +39,11 @@ def tile_list_panel_programme_features_kernel(
     with ExitStack() as ctx:
         lists = ctx.enter_context(tc.tile_pool(name="lists", bufs=1))
         keep = ctx.enter_context(tc.tile_pool(name="keep", bufs=1))
-        ring = ctx.enter_context(tc.tile_pool(name="ring", bufs=3))
+        ring = ctx.enter_context(tc.tile_pool(name="ring", bufs=4))
         pair = ctx.enter_context(tc.tile_pool(name="pair", bufs=2))
+        split = ctx.enter_context(tc.tile_pool(name="split", bufs=2))
         sums = ctx.enter_context(tc.psum_pool(name="sums", bufs=4))
-        turned = ctx.enter_context(tc.psum_pool(name="turned", bufs=3))
+        turned = ctx.enter_context(tc.psum_pool(name="turned", bufs=4))
 
         def load_list(src, name):
             held = lists.tile(list(src.shape), U16, name=name)
@@ -65,17 +66,17 @@ def tile_list_panel_programme_features_kernel(
         nc.vector.memset(w4_plane[:].bitcast(I32), 0)
 
         idx = load_list(offs, "idx")
-        w1_raw = [load_w1(0)]
         for q in range(4):
             nc.sync.dma_start(
                 table_scales[32 * q : 32 * q + 4 * PASSES, :].bitcast(I32),
                 tab_scales[:, 4 * q : 4 * q + 4, :].bitcast(I32),
             )
-        table_words = [load_words(0)]
-        w1_raw.append(load_w1(1))
-        table_words.append(load_words(1))
         p2 = load_list(pos2, "p2")
         p1 = load_list(pos1, "p1")
+        w1_raw, table_words = [], []
+        for a in range(PASSES):
+            w1_raw.append(load_w1(a))
+            table_words.append(load_words(a))
         p3 = load_list(pos3, "p3")
         p4 = load_list(pos4, "p4")
         p5 = load_list(pos5, "p5")
@@ -98,7 +99,7 @@ def tile_list_panel_programme_features_kernel(
 
         def quantise_w1(a):
             grouped = keep.tile([P, H * PACK], BF16, name="w1_grouped%d" % a, align_bytes=64)
-            nc.scalar.copy(
+            nc.vector.tensor_copy(
                 grouped[:].rearrange("p (t m j) -> p m j t", t=PACK, j=PACK),
                 w1_raw[a][:].rearrange("p j (m t) -> p m j t", t=PACK),
             )
@@ -126,36 +127,78 @@ def tile_list_panel_programme_features_kernel(
         h = [keep.tile([P, S], F32, name="h%d" % t) for t in range(PACK)]
         a3 = keep.tile([P, PACK, P3], F32, name="a3")
 
-        def features(t, c):
-            x = sums.tile([P, CHUNK], F32, name="x", tag="sums")
+        to_bits = -BITS_PER_TURN / (2.0 * math.pi)
+        to_turns = 1.0 / (2.0 * math.pi)
+
+        def features_by_transposes(t, c0):
             rows = slice(t * P, (t + 1) * P)
-            for b in range(BLOCKS):
-                picks = slice(c * CHUNK + b * P, c * CHUNK + (b + 1) * P)
+            banks = []
+            for c in (c0, c0 + 1):
+                x = sums.tile([P, CHUNK], F32, name="x", tag="sums")
+                for b in range(BLOCKS):
+                    picks = slice(c * CHUNK + b * P, c * CHUNK + (b + 1) * P)
+                    for a in range(PASSES):
+                        nc.tensor.matmul_mx(
+                            out=x[:, b * P : (b + 1) * P],
+                            lhsT=picked_words[a][:, picks].bitcast(FP8X4),
+                            lhsT_scale=picked_scales[4 * a :, picks],
+                            rhs=w1_codes[a][:, rows].bitcast(FP8X4),
+                            rhs_scale=w1_planes[a][:, rows],
+                            start=(a == 0),
+                            stop=(a == PASSES - 1),
+                        )
+                banks.append(x)
+            parts = split.tile([P, 4 * CHUNK], U32, name="parts", tag="split")
+            whole = [parts[:, i * CHUNK : (i + 1) * CHUNK] for i in range(2)]
+            turns = [parts[:, (2 + i) * CHUNK : (3 + i) * CHUNK].bitcast(F32) for i in range(2)]
+            for i in (0, 1):
+                nc.scalar.activation(whole[i], banks[i][:], ACT.Copy, scale=to_bits, bias=TURN_BASE_BITS)
+            for i in (1, 0):
+                nc.scalar.activation(turns[i], banks[i][:], ACT.Copy, scale=to_turns)
+            for i in (1, 0):
+                rest = turned.tile([P, CHUNK], F32, name="rest")
+                for b in range(BLOCKS):
+                    blk = slice(b * P, (b + 1) * P)
+                    terms = (minus_base[:], whole[i][:, blk].bitcast(F32), turns[i][:, blk])
+                    for n, term in enumerate(terms):
+                        nc.tensor.matmul(
+                            rest[:, blk], term, identity[:], is_transpose=True, start=(n == 0), stop=(n == 2)
+                        )
+                picks = slice((c0 + i) * CHUNK, (c0 + i + 1) * CHUNK)
+                nc.scalar.activation(h[t][:, picks], rest[:], ACT.Sin, scale=2.0 * math.pi)
+
+        def first_features():
+            early = (CHUNKS - 1) * CHUNK
+            rest_early = split.tile([P, early], F32, name="rest_early", tag="split")
+            rest_last = split.tile([P, CHUNK], F32, name="rest_last", tag="split")
+            for c in range(CHUNKS):
+                last = c == CHUNKS - 1
+                x = sums.tile([P, CHUNK], F32, name="x", tag="sums")
+                picks = slice(c * CHUNK, (c + 1) * CHUNK)
                 for a in range(PASSES):
                     nc.tensor.matmul_mx(
-                        out=x[:, b * P : (b + 1) * P],
-                        lhsT=picked_words[a][:, picks].bitcast(FP8X4),
-                        lhsT_scale=picked_scales[4 * a :, picks],
-                        rhs=w1_codes[a][:, rows].bitcast(FP8X4),
-                        rhs_scale=w1_planes[a][:, rows],
+                        out=x[:],
+                        lhsT=w1_codes[a][:, :P].bitcast(FP8X4),
+                        lhsT_scale=w1_planes[a][:, :P],
+                        rhs=picked_words[a][:, picks].bitcast(FP8X4),
+                        rhs_scale=picked_scales[4 * a :, picks],
                         start=(a == 0),
                         stop=(a == PASSES - 1),
                     )
-            whole = ring.tile([P, CHUNK], U32, name="whole")
-            nc.scalar.activation(
-                whole[:], x[:], ACT.Copy, scale=-BITS_PER_TURN / (2.0 * math.pi), bias=TURN_BASE_BITS
-            )
-            turns = ring.tile([P, CHUNK], F32, name="turns")
-            nc.scalar.activation(turns[:], x[:], ACT.Copy, scale=1.0 / (2.0 * math.pi))
-            rest = turned.tile([P, CHUNK], F32, name="rest")
-            for b in range(BLOCKS):
-                blk = slice(b * P, (b + 1) * P)
-                terms = (minus_base[:], whole[:, blk].bitcast(F32), turns[:, blk])
-                for i, term in enumerate(terms):
-                    nc.tensor.matmul(
-                        rest[:, blk], term, identity[:], is_transpose=True, start=(i == 0), stop=(i == len(terms) - 1)
-                    )
-            nc.scalar.activation(h[t][:, c * CHUNK : (c + 1) * CHUNK], rest[:], ACT.Sin, scale=2.0 * math.pi)
+                turns = ring.tile([P, CHUNK], F32, name="turns")
+                nc.scalar.activation(turns[:], x[:], ACT.Copy, scale=to_turns)
+                whole = ring.tile([P, CHUNK], U32, name="whole")
+                if last:
+                    nc.vector.tensor_scalar(whole[:].bitcast(I32), x[:], to_bits, TURN_BASE_BITS, ALU.mult, ALU.add)
+                else:
+                    nc.scalar.activation(whole[:], x[:], ACT.Copy, scale=to_bits, bias=TURN_BASE_BITS)
+                rest = rest_last[:] if last else rest_early[:, picks]
+                nc.vector.scalar_tensor_tensor(
+                    rest, whole[:].bitcast(F32), TURN_BASE, turns[:], ALU.subtract, ALU.add
+                )
+                if c == CHUNKS - 2:
+                    nc.scalar.activation(h[0][:, :early], rest_early[:], ACT.Sin, scale=2.0 * math.pi)
+            nc.scalar.activation(h[0][:, early:], rest_last[:], ACT.Sin, scale=2.0 * math.pi)
 
         def levels(t):
             right = pair.tile([P, P1], F32, name="right")
@@ -181,9 +224,11 @@ def tile_list_panel_programme_features_kernel(
             nc.vector.tensor_copy(term[:], a2[:].indirect(p5[:]))
             nc.vector.tensor_tensor(a3[:, t, :], a2[:].indirect(p6[:]), term[:], ALU.add)
 
-        for t in range(PACK):
-            for c in range(CHUNKS):
-                features(t, c)
+        first_features()
+        levels(0)
+        for t in range(1, PACK):
+            for c0 in range(0, CHUNKS, 2):
+                features_by_transposes(t, c0)
             levels(t)
 
         a3_grouped = keep.tile([P, P3, PACK], BF16, name="a3_grouped", align_bytes=64)
@@ -199,20 +244,17 @@ def tile_list_panel_programme_features_kernel(
             out=a3_codes[:].bitcast(FP8X4), scales=a3_plane[:], in_=a3_grouped[:].rearrange("p j t -> p (j t)")
         )
 
-        out_rows = out.rearrange("(b p) j -> p b j", p=P)
-        for bank in range(2):
-            y = sums.tile([P, 2, P3], F32, name="y", tag="sums")
-            for i in range(2):
-                b = 2 * bank + i
-                nc.tensor.matmul_mx(
-                    out=y[:, i, :],
-                    lhsT=w4_codes[:, 2 * P * b : 2 * P * (b + 1)].bitcast(FP4X4),
-                    lhsT_scale=w4_plane[:, P * b : P * (b + 1)],
-                    rhs=a3_codes[:].bitcast(FP8X4),
-                    rhs_scale=a3_plane[:],
-                    start=True,
-                    stop=True,
-                )
-            scores = pair.tile([P, 2, P3], F32, name="scores")
+        for b in range(N // P):
+            y = sums.tile([P, P3], F32, name="y", tag="sums")
+            nc.tensor.matmul_mx(
+                out=y[:],
+                lhsT=w4_codes[:, 2 * P * b : 2 * P * (b + 1)].bitcast(FP4X4),
+                lhsT_scale=w4_plane[:, P * b : P * (b + 1)],
+                rhs=a3_codes[:].bitcast(FP8X4),
+                rhs_scale=a3_plane[:],
+                start=True,
+                stop=True,
+            )
+            scores = ring.tile([P, P3], F32, name="scores")
             nc.scalar.activation(scores[:], y[:], ACT.Sigmoid)
-            nc.sync.dma_start(out_rows[:, 2 * bank : 2 * bank + 2, :], scores[:])
+            nc.sync.dma_start(out[P * b : P * (b + 1), :], scores[:])

@@ -27,9 +27,7 @@ CHUNKS = S // CHUNK
 BLOCKS = CHUNK // P
 LIST_ROWS = 16
 
-TURN_BASE = 98304.0
-TURN_BASE_BITS = float(0x47C00000)
-BITS_PER_TURN = 128.0
+ROUNDER = 1.5 * 2.0**23
 
 
 def tile_list_panel_programme_features_kernel(
@@ -92,8 +90,8 @@ def tile_list_panel_programme_features_kernel(
 
         identity = keep.tile([P, P], F32, name="identity")
         make_identity(nc, identity[:])
-        minus_base = keep.tile([P, P], F32, name="minus_base")
-        nc.gpsimd.memset(minus_base[:], -TURN_BASE)
+        warm = keep.tile([P, 1], F32, name="warm")
+        nc.scalar.activation(warm[:], identity[:, :1], ACT.Sin)
 
         w1_codes, w1_planes = [], []
 
@@ -127,7 +125,6 @@ def tile_list_panel_programme_features_kernel(
         h = [keep.tile([P, S], F32, name="h%d" % t) for t in range(PACK)]
         a3 = keep.tile([P, PACK, P3], F32, name="a3")
 
-        to_bits = -BITS_PER_TURN / (2.0 * math.pi)
         to_turns = 1.0 / (2.0 * math.pi)
 
         def features_by_transposes(t, c0):
@@ -148,21 +145,27 @@ def tile_list_panel_programme_features_kernel(
                             stop=(a == PASSES - 1),
                         )
                 banks.append(x)
-            parts = split.tile([P, 4 * CHUNK], U32, name="parts", tag="split")
-            whole = [parts[:, i * CHUNK : (i + 1) * CHUNK] for i in range(2)]
-            turns = [parts[:, (2 + i) * CHUNK : (3 + i) * CHUNK].bitcast(F32) for i in range(2)]
-            for i in (0, 1):
-                nc.scalar.activation(whole[i], banks[i][:], ACT.Copy, scale=to_bits, bias=TURN_BASE_BITS)
-            for i in (1, 0):
-                nc.scalar.activation(turns[i], banks[i][:], ACT.Copy, scale=to_turns)
-            for i in (1, 0):
+            parts = split.tile([P, 6 * CHUNK], U32, name="parts", tag="split")
+            shifted = parts[:, : 2 * CHUNK]
+            turns = parts[:, 2 * CHUNK : 4 * CHUNK].bitcast(F32)
+            minus_whole = parts[:, 4 * CHUNK :].bitcast(F32)
+            for i, x in enumerate(banks):
+                own = slice(i * CHUNK, (i + 1) * CHUNK)
+                nc.scalar.activation(shifted[:, own], x[:], ACT.Copy, scale=to_turns, bias=ROUNDER)
+                nc.scalar.activation(turns[:, own], x[:], ACT.Copy, scale=to_turns)
+            nc.scalar.activation(minus_whole, shifted, ACT.Copy, scale=-1.0, bias=ROUNDER)
+            for i in range(2):
                 rest = turned.tile([P, CHUNK], F32, name="rest")
                 for b in range(BLOCKS):
-                    blk = slice(b * P, (b + 1) * P)
-                    terms = (minus_base[:], whole[i][:, blk].bitcast(F32), turns[i][:, blk])
-                    for n, term in enumerate(terms):
+                    blk = slice(i * CHUNK + b * P, i * CHUNK + (b + 1) * P)
+                    for n, term in enumerate((minus_whole, turns)):
                         nc.tensor.matmul(
-                            rest[:, blk], term, identity[:], is_transpose=True, start=(n == 0), stop=(n == 2)
+                            rest[:, b * P : (b + 1) * P],
+                            term[:, blk],
+                            identity[:],
+                            is_transpose=True,
+                            start=(n == 0),
+                            stop=(n == 1),
                         )
                 picks = slice((c0 + i) * CHUNK, (c0 + i + 1) * CHUNK)
                 nc.scalar.activation(h[t][:, picks], rest[:], ACT.Sin, scale=2.0 * math.pi)
@@ -187,18 +190,18 @@ def tile_list_panel_programme_features_kernel(
                     )
                 turns = ring.tile([P, CHUNK], F32, name="turns")
                 nc.scalar.activation(turns[:], x[:], ACT.Copy, scale=to_turns)
-                whole = ring.tile([P, CHUNK], U32, name="whole")
+                shifted = ring.tile([P, CHUNK], U32, name="shifted")
                 if last:
-                    nc.vector.tensor_scalar(whole[:].bitcast(I32), x[:], to_bits, TURN_BASE_BITS, ALU.mult, ALU.add)
+                    nc.vector.tensor_scalar(shifted[:].bitcast(I32), x[:], to_turns, ROUNDER, ALU.mult, ALU.add)
                 else:
-                    nc.scalar.activation(whole[:], x[:], ACT.Copy, scale=to_bits, bias=TURN_BASE_BITS)
+                    nc.scalar.activation(shifted[:], x[:], ACT.Copy, scale=to_turns, bias=ROUNDER)
                 rest = rest_last[:] if last else rest_early[:, picks]
                 nc.vector.scalar_tensor_tensor(
-                    rest, whole[:].bitcast(F32), TURN_BASE, turns[:], ALU.subtract, ALU.add
+                    rest, shifted[:].bitcast(I32), ROUNDER, turns[:], ALU.subtract, ALU.subtract
                 )
                 if c == CHUNKS - 2:
-                    nc.scalar.activation(h[0][:, :early], rest_early[:], ACT.Sin, scale=2.0 * math.pi)
-            nc.scalar.activation(h[0][:, early:], rest_last[:], ACT.Sin, scale=2.0 * math.pi)
+                    nc.scalar.activation(h[0][:, :early], rest_early[:], ACT.Sin, scale=-2.0 * math.pi)
+            nc.scalar.activation(h[0][:, early:], rest_last[:], ACT.Sin, scale=-2.0 * math.pi)
 
         def levels(t):
             right = pair.tile([P, P1], F32, name="right")

@@ -39,7 +39,7 @@ def tile_list_panel_programme_features_kernel(
         keep = ctx.enter_context(tc.tile_pool(name="keep", bufs=1))
         ring = ctx.enter_context(tc.tile_pool(name="ring", bufs=4))
         pair = ctx.enter_context(tc.tile_pool(name="pair", bufs=2))
-        split = ctx.enter_context(tc.tile_pool(name="split", bufs=2))
+        split = ctx.enter_context(tc.tile_pool(name="split", bufs=1))
         sums = ctx.enter_context(tc.psum_pool(name="sums", bufs=4))
         turned = ctx.enter_context(tc.psum_pool(name="turned", bufs=4))
 
@@ -71,10 +71,8 @@ def tile_list_panel_programme_features_kernel(
             )
         p2 = load_list(pos2, "p2")
         p1 = load_list(pos1, "p1")
-        w1_raw, table_words = [], []
-        for a in range(PASSES):
-            w1_raw.append(load_w1(a))
-            table_words.append(load_words(a))
+        w1_raw = [load_w1(a) for a in range(PASSES)]
+        table_words = [load_words(a) for a in range(PASSES)]
         p3 = load_list(pos3, "p3")
         p4 = load_list(pos4, "p4")
         p5 = load_list(pos5, "p5")
@@ -93,34 +91,31 @@ def tile_list_panel_programme_features_kernel(
         warm = keep.tile([P, 1], F32, name="warm")
         nc.scalar.activation(warm[:], identity[:, :1], ACT.Sin)
 
-        w1_codes, w1_planes = [], []
-
-        def quantise_w1(a):
-            grouped = keep.tile([P, H * PACK], BF16, name="w1_grouped%d" % a, align_bytes=64)
-            nc.vector.tensor_copy(
-                grouped[:].rearrange("p (t m j) -> p m j t", t=PACK, j=PACK),
-                w1_raw[a][:].rearrange("p j (m t) -> p m j t", t=PACK),
-            )
-            codes = keep.tile([P, H], U32, name="w1_codes%d" % a, align_bytes=64)
-            plane = keep.tile([P, H], U8, name="w1_plane%d" % a, align_bytes=64)
-            nc.vector.quantize_mx(out=codes[:].bitcast(FP8X4), scales=plane[:], in_=grouped[:])
-            w1_codes.append(codes)
-            w1_planes.append(plane)
-
         picked_scales = keep.tile([P, S], U8, name="picked_scales", align_bytes=64)
         nc.vector.tensor_copy(picked_scales[:], table_scales[:].indirect(idx[:]))
-        quantise_w1(0)
-        picked0 = keep.tile([P, S], U32, name="picked_words0", align_bytes=64)
-        nc.vector.tensor_copy(picked0[:], table_words[0][:].bitcast(U32).indirect(idx[:]))
-        quantise_w1(1)
-        picked1 = keep.tile([P, S], U32, name="picked_words1", align_bytes=64)
-        cols = CHUNK // LIST_ROWS
-        for c in range(CHUNKS):
+
+        grouped = keep.tile([P, PASSES * H * PACK], BF16, name="w1_grouped", tag="staged", align_bytes=64)
+        for a in range(PASSES):
             nc.vector.tensor_copy(
-                picked1[:, c * CHUNK : (c + 1) * CHUNK],
-                table_words[1][:].bitcast(U32).indirect(idx[:, c * cols : (c + 1) * cols]),
+                grouped[:, a * H * PACK : (a + 1) * H * PACK].rearrange("p (t m j) -> p m j t", t=PACK, j=PACK),
+                w1_raw[a][:].rearrange("p j (m t) -> p m j t", t=PACK),
             )
-        picked_words = [picked0, picked1]
+        codes = keep.tile([P, PASSES * H], U32, name="w1_codes", align_bytes=64)
+        plane = keep.tile([P, PASSES * H], U8, name="w1_plane", align_bytes=64)
+        nc.vector.quantize_mx(out=codes[:].bitcast(FP8X4), scales=plane[:], in_=grouped[:])
+        w1_codes = [codes[:, a * H : (a + 1) * H] for a in range(PASSES)]
+        w1_planes = [plane[:, a * H : (a + 1) * H] for a in range(PASSES)]
+
+        picked_words = [
+            keep.tile([P, S], U32, name="picked_words0", tag="staged", align_bytes=64),
+            keep.tile([P, S], U32, name="picked_words1", align_bytes=64),
+        ]
+        for a, width in enumerate((2 * CHUNK, CHUNK)):
+            for start in range(0, S, width):
+                nc.vector.tensor_copy(
+                    picked_words[a][:, start : start + width],
+                    table_words[a][:].bitcast(U32).indirect(idx[:, start // LIST_ROWS : (start + width) // LIST_ROWS]),
+                )
 
         h = [keep.tile([P, S], F32, name="h%d" % t) for t in range(PACK)]
         a3 = keep.tile([P, PACK, P3], F32, name="a3")
@@ -145,7 +140,7 @@ def tile_list_panel_programme_features_kernel(
                             stop=(a == PASSES - 1),
                         )
                 banks.append(x)
-            parts = split.tile([P, 6 * CHUNK], U32, name="parts", tag="split")
+            parts = split.tile([P, 6 * CHUNK], U32, name="parts", tag="split%d" % (c0 // 2))
             shifted = parts[:, : 2 * CHUNK]
             turns = parts[:, 2 * CHUNK : 4 * CHUNK].bitcast(F32)
             minus_whole = parts[:, 4 * CHUNK :].bitcast(F32)
@@ -172,8 +167,8 @@ def tile_list_panel_programme_features_kernel(
 
         def first_features():
             early = (CHUNKS - 1) * CHUNK
-            rest_early = split.tile([P, early], F32, name="rest_early", tag="split")
-            rest_last = split.tile([P, CHUNK], F32, name="rest_last", tag="split")
+            rest_early = split.tile([P, early], F32, name="rest_early", tag="split0")
+            rest_last = split.tile([P, CHUNK], F32, name="rest_last", tag="split1")
             for c in range(CHUNKS):
                 last = c == CHUNKS - 1
                 x = sums.tile([P, CHUNK], F32, name="x", tag="sums")
@@ -235,11 +230,13 @@ def tile_list_panel_programme_features_kernel(
             levels(t)
 
         a3_grouped = keep.tile([P, P3, PACK], BF16, name="a3_grouped", align_bytes=64)
-        nc.vector.tensor_tensor(
-            a3_grouped[:],
-            a3[:].rearrange("p t j -> p j t"),
-            gains[:].unsqueeze(1).to_broadcast([P, P3, PACK]),
-            ALU.mult,
+        scaled = split.tile([P, PACK, P3], F32, name="scaled", tag="split1")
+        for t in range(PACK - 1):
+            nc.scalar.activation(scaled[:, t, :], a3[:, t, :], ACT.Copy, scale=gains[:, t : t + 1])
+        nc.vector.tensor_scalar_mul(scaled[:, PACK - 1, :], a3[:, PACK - 1, :], gains[:, PACK - 1 :])
+        nc.vector.tensor_copy(
+            a3_grouped[:].rearrange("p (c i) t -> p c t i", i=PACK),
+            scaled[:].rearrange("p t (c i) -> p c t i", i=PACK),
         )
         a3_codes = keep.tile([P, P3], U32, name="a3_codes", align_bytes=64)
         a3_plane = keep.tile([P, P3], U8, name="a3_plane", align_bytes=64)

@@ -26,8 +26,11 @@ CHUNK = 512
 CHUNKS = S // CHUNK
 BLOCKS = CHUNK // P
 LIST_ROWS = 16
+HALVES = 2
 
-ROUNDER = 1.5 * 2.0**23
+TURN_BASE = 98304.0
+TURN_BASE_BITS = float(0x47C00000)
+BITS_PER_TURN = 128.0
 
 
 def tile_list_panel_programme_features_kernel(
@@ -71,8 +74,10 @@ def tile_list_panel_programme_features_kernel(
             )
         p2 = load_list(pos2, "p2")
         p1 = load_list(pos1, "p1")
-        w1_raw = [load_w1(a) for a in range(PASSES)]
-        table_words = [load_words(a) for a in range(PASSES)]
+        w1_raw, table_words = [], []
+        for a in range(PASSES):
+            w1_raw.append(load_w1(a))
+            table_words.append(load_words(a))
         p3 = load_list(pos3, "p3")
         p4 = load_list(pos4, "p4")
         p5 = load_list(pos5, "p5")
@@ -88,29 +93,25 @@ def tile_list_panel_programme_features_kernel(
 
         identity = keep.tile([P, P], F32, name="identity")
         make_identity(nc, identity[:])
+        minus_base = keep.tile([P, P], F32, name="minus_base")
+        nc.gpsimd.memset(minus_base[:], -TURN_BASE)
         warm = keep.tile([P, 1], F32, name="warm")
         nc.scalar.activation(warm[:], identity[:, :1], ACT.Sin)
 
         picked_scales = keep.tile([P, S], U8, name="picked_scales", align_bytes=64)
         nc.vector.tensor_copy(picked_scales[:], table_scales[:].indirect(idx[:]))
 
-        grouped = keep.tile([P, PASSES * H * PACK], BF16, name="w1_grouped", tag="staged", align_bytes=64)
-        for a in range(PASSES):
-            nc.vector.tensor_copy(
-                grouped[:, a * H * PACK : (a + 1) * H * PACK].rearrange("p (t m j) -> p m j t", t=PACK, j=PACK),
+        w1_codes, w1_planes, picked_words = [], [], []
+        for a, (interleave, width) in enumerate(((nc.vector.tensor_copy, S), (nc.scalar.copy, CHUNK))):
+            grouped = keep.tile([P, H * PACK], BF16, name="w1_grouped", tag="staged%d" % a, align_bytes=64)
+            interleave(
+                grouped[:].rearrange("p (t m j) -> p m j t", t=PACK, j=PACK),
                 w1_raw[a][:].rearrange("p j (m t) -> p m j t", t=PACK),
             )
-        codes = keep.tile([P, PASSES * H], U32, name="w1_codes", align_bytes=64)
-        plane = keep.tile([P, PASSES * H], U8, name="w1_plane", align_bytes=64)
-        nc.vector.quantize_mx(out=codes[:].bitcast(FP8X4), scales=plane[:], in_=grouped[:])
-        w1_codes = [codes[:, a * H : (a + 1) * H] for a in range(PASSES)]
-        w1_planes = [plane[:, a * H : (a + 1) * H] for a in range(PASSES)]
-
-        picked_words = [
-            keep.tile([P, S], U32, name="picked_words0", tag="staged", align_bytes=64),
-            keep.tile([P, S], U32, name="picked_words1", align_bytes=64),
-        ]
-        for a, width in enumerate((2 * CHUNK, CHUNK)):
+            w1_codes.append(keep.tile([P, H], U32, name="w1_codes%d" % a, align_bytes=64))
+            w1_planes.append(keep.tile([P, H], U8, name="w1_plane%d" % a, align_bytes=64))
+            nc.vector.quantize_mx(out=w1_codes[a][:].bitcast(FP8X4), scales=w1_planes[a][:], in_=grouped[:])
+            picked_words.append(keep.tile([P, S], U32, name="picked_words", tag="staged%d" % a, align_bytes=64))
             for start in range(0, S, width):
                 nc.vector.tensor_copy(
                     picked_words[a][:, start : start + width],
@@ -120,6 +121,7 @@ def tile_list_panel_programme_features_kernel(
         h = [keep.tile([P, S], F32, name="h%d" % t) for t in range(PACK)]
         a3 = keep.tile([P, PACK, P3], F32, name="a3")
 
+        to_bits = -BITS_PER_TURN / (2.0 * math.pi)
         to_turns = 1.0 / (2.0 * math.pi)
 
         def features_by_transposes(t, c0):
@@ -140,27 +142,21 @@ def tile_list_panel_programme_features_kernel(
                             stop=(a == PASSES - 1),
                         )
                 banks.append(x)
-            parts = split.tile([P, 6 * CHUNK], U32, name="parts", tag="split%d" % (c0 // 2))
-            shifted = parts[:, : 2 * CHUNK]
-            turns = parts[:, 2 * CHUNK : 4 * CHUNK].bitcast(F32)
-            minus_whole = parts[:, 4 * CHUNK :].bitcast(F32)
-            for i, x in enumerate(banks):
-                own = slice(i * CHUNK, (i + 1) * CHUNK)
-                nc.scalar.activation(shifted[:, own], x[:], ACT.Copy, scale=to_turns, bias=ROUNDER)
-                nc.scalar.activation(turns[:, own], x[:], ACT.Copy, scale=to_turns)
-            nc.scalar.activation(minus_whole, shifted, ACT.Copy, scale=-1.0, bias=ROUNDER)
-            for i in range(2):
+            parts = split.tile([P, 4 * CHUNK], U32, name="parts", tag="split%d" % (c0 // 2))
+            whole = [parts[:, i * CHUNK : (i + 1) * CHUNK] for i in range(2)]
+            turns = [parts[:, (2 + i) * CHUNK : (3 + i) * CHUNK].bitcast(F32) for i in range(2)]
+            for i in (0, 1):
+                nc.scalar.activation(whole[i], banks[i][:], ACT.Copy, scale=to_bits, bias=TURN_BASE_BITS)
+            for i in (1, 0):
+                nc.scalar.activation(turns[i], banks[i][:], ACT.Copy, scale=to_turns)
+            for i in (1, 0):
                 rest = turned.tile([P, CHUNK], F32, name="rest")
                 for b in range(BLOCKS):
-                    blk = slice(i * CHUNK + b * P, i * CHUNK + (b + 1) * P)
-                    for n, term in enumerate((minus_whole, turns)):
+                    blk = slice(b * P, (b + 1) * P)
+                    terms = (minus_base[:], whole[i][:, blk].bitcast(F32), turns[i][:, blk])
+                    for n, term in enumerate(terms):
                         nc.tensor.matmul(
-                            rest[:, b * P : (b + 1) * P],
-                            term[:, blk],
-                            identity[:],
-                            is_transpose=True,
-                            start=(n == 0),
-                            stop=(n == 1),
+                            rest[:, blk], term, identity[:], is_transpose=True, start=(n == 0), stop=(n == 2)
                         )
                 picks = slice((c0 + i) * CHUNK, (c0 + i + 1) * CHUNK)
                 nc.scalar.activation(h[t][:, picks], rest[:], ACT.Sin, scale=2.0 * math.pi)
@@ -185,42 +181,63 @@ def tile_list_panel_programme_features_kernel(
                     )
                 turns = ring.tile([P, CHUNK], F32, name="turns")
                 nc.scalar.activation(turns[:], x[:], ACT.Copy, scale=to_turns)
-                shifted = ring.tile([P, CHUNK], U32, name="shifted")
+                whole = ring.tile([P, CHUNK], U32, name="whole")
                 if last:
-                    nc.vector.tensor_scalar(shifted[:].bitcast(I32), x[:], to_turns, ROUNDER, ALU.mult, ALU.add)
+                    nc.vector.tensor_scalar(whole[:].bitcast(I32), x[:], to_bits, TURN_BASE_BITS, ALU.mult, ALU.add)
                 else:
-                    nc.scalar.activation(shifted[:], x[:], ACT.Copy, scale=to_turns, bias=ROUNDER)
+                    nc.scalar.activation(whole[:], x[:], ACT.Copy, scale=to_bits, bias=TURN_BASE_BITS)
                 rest = rest_last[:] if last else rest_early[:, picks]
                 nc.vector.scalar_tensor_tensor(
-                    rest, shifted[:].bitcast(I32), ROUNDER, turns[:], ALU.subtract, ALU.subtract
+                    rest, whole[:].bitcast(F32), TURN_BASE, turns[:], ALU.subtract, ALU.add
                 )
                 if c == CHUNKS - 2:
-                    nc.scalar.activation(h[0][:, :early], rest_early[:], ACT.Sin, scale=-2.0 * math.pi)
-            nc.scalar.activation(h[0][:, early:], rest_last[:], ACT.Sin, scale=-2.0 * math.pi)
+                    nc.scalar.activation(h[0][:, :early], rest_early[:], ACT.Sin, scale=2.0 * math.pi)
+            nc.scalar.activation(h[0][:, early:], rest_last[:], ACT.Sin, scale=2.0 * math.pi)
+
+        def picks_of(held, start, width):
+            return held[:, start // LIST_ROWS : (start + width) // LIST_ROWS]
+
+        a2 = []
+
+        def last_level_first_term(t, pieces):
+            term = pair.tile([P, P3], F32, name="term", tag="right0", bufs=1)
+            width = P3 // pieces
+            for start in range(0, P3, width):
+                nc.vector.tensor_copy(term[:, start : start + width], a2[t][:].indirect(picks_of(p5, start, width)))
+            return term
+
+        def last_level_sum(t, term, pieces):
+            width = P3 // pieces
+            for start in range(0, P3, width):
+                own = slice(start, start + width)
+                nc.vector.tensor_tensor(
+                    a3[:, t, own], a2[t][:].indirect(picks_of(p6, start, width)), term[:, own], ALU.add
+                )
 
         def levels(t):
-            right = pair.tile([P, P1], F32, name="right")
             half = P1 // 2
+            right = [pair.tile([P, half], F32, name="right", tag="right%d" % s, bufs=1) for s in range(2)]
             for s in range(2):
                 nc.vector.tensor_scalar(
-                    right[:, s * half : (s + 1) * half],
-                    h[t][:].indirect(p2[:, s * half // LIST_ROWS : (s + 1) * half // LIST_ROWS]),
-                    1.0,
-                    1.0,
-                    ALU.mult,
-                    ALU.add,
+                    right[s][:], h[t][:].indirect(picks_of(p2, s * half, half)), 1.0, 1.0, ALU.mult, ALU.add
                 )
             a1 = pair.tile([P, P1], F32, name="a1")
-            nc.vector.tensor_tensor(a1[:], h[t][:].indirect(p1[:]), right[:], ALU.mult)
+            for s in range(2):
+                nc.vector.tensor_tensor(
+                    a1[:, s * half : (s + 1) * half],
+                    h[t][:].indirect(picks_of(p1, s * half, half)),
+                    right[s][:],
+                    ALU.mult,
+                )
+            term = last_level_first_term(t - 1, 1) if t else None
             first = pair.tile([P, P2], F32, name="first")
             second = pair.tile([P, P2], F32, name="second")
             nc.vector.tensor_copy(first[:], a1[:].indirect(p3[:]))
             nc.vector.tensor_copy(second[:], a1[:].indirect(p4[:]))
-            a2 = pair.tile([P, P2], F32, name="a2")
-            nc.vector.tensor_tensor(a2[:], first[:], second[:], ALU.min)
-            term = pair.tile([P, P3], F32, name="term")
-            nc.vector.tensor_copy(term[:], a2[:].indirect(p5[:]))
-            nc.vector.tensor_tensor(a3[:, t, :], a2[:].indirect(p6[:]), term[:], ALU.add)
+            if t:
+                last_level_sum(t - 1, term, 1)
+            a2.append(pair.tile([P, P2], F32, name="a2"))
+            nc.vector.tensor_tensor(a2[t][:], first[:], second[:], ALU.min)
 
         first_features()
         levels(0)
@@ -228,21 +245,28 @@ def tile_list_panel_programme_features_kernel(
             for c0 in range(0, CHUNKS, 2):
                 features_by_transposes(t, c0)
             levels(t)
+        last_level_sum(PACK - 1, last_level_first_term(PACK - 1, HALVES), HALVES)
 
-        a3_grouped = keep.tile([P, P3, PACK], BF16, name="a3_grouped", align_bytes=64)
+        halves = [slice(i * P3 // HALVES, (i + 1) * P3 // HALVES) for i in range(HALVES)]
         scaled = split.tile([P, PACK, P3], F32, name="scaled", tag="split1")
         for t in range(PACK - 1):
             nc.scalar.activation(scaled[:, t, :], a3[:, t, :], ACT.Copy, scale=gains[:, t : t + 1])
-        nc.vector.tensor_scalar_mul(scaled[:, PACK - 1, :], a3[:, PACK - 1, :], gains[:, PACK - 1 :])
-        nc.vector.tensor_copy(
-            a3_grouped[:].rearrange("p (c i) t -> p c t i", i=PACK),
-            scaled[:].rearrange("p t (c i) -> p c t i", i=PACK),
-        )
+        for own in halves:
+            nc.vector.tensor_scalar_mul(scaled[:, PACK - 1, own], a3[:, PACK - 1, own], gains[:, PACK - 1 :])
+        a3_grouped = keep.tile([P, P3, PACK], BF16, name="a3_grouped", align_bytes=64)
+        for own in halves:
+            nc.vector.tensor_copy(
+                a3_grouped[:, own, :].rearrange("p (c i) t -> p c t i", i=PACK),
+                scaled[:, :, own].rearrange("p t (c i) -> p c t i", i=PACK),
+            )
         a3_codes = keep.tile([P, P3], U32, name="a3_codes", align_bytes=64)
         a3_plane = keep.tile([P, P3], U8, name="a3_plane", align_bytes=64)
-        nc.vector.quantize_mx(
-            out=a3_codes[:].bitcast(FP8X4), scales=a3_plane[:], in_=a3_grouped[:].rearrange("p j t -> p (j t)")
-        )
+        for own in halves:
+            nc.vector.quantize_mx(
+                out=a3_codes[:, own].bitcast(FP8X4),
+                scales=a3_plane[:, own],
+                in_=a3_grouped[:, own, :].rearrange("p j t -> p (j t)"),
+            )
 
         for b in range(N // P):
             y = sums.tile([P, P3], F32, name="y", tag="sums")

import math
from contextlib import ExitStack

import concourse.mybir as mybir
from concourse.masks import make_identity

K, H, N, T, S = 1024, 512, 512, 4096, 2048
P1, P2, P3 = 1024, 512, 256
FLOPS = 2 * K * H * S + 2 * H * N * P3

F32 = mybir.dt.float32
BF16 = mybir.dt.bfloat16
I32 = mybir.dt.int32
U32 = mybir.dt.uint32
U16 = mybir.dt.uint16
U8 = mybir.dt.uint8
FP8X4 = mybir.dt.float8_e4m3fn_x4
FP4X4 = mybir.dt.float4_e2m1fn_x4
ALU = mybir.AluOpType
ACT = mybir.ActivationFunctionType

P = 128
PACK = 4
PASSES = K // (P * PACK)
CHUNK = 512
CHUNKS = S // CHUNK
BLOCKS = CHUNK // P
LIST_ROWS = 16
HALVES = 2

TURN_BASE = 98304.0
TURN_BASE_BITS = float(0x47C00000)
BITS_PER_TURN = 128.0


def tile_list_panel_programme_features_kernel(
    tc, tab_words, tab_scales, offs, pos1, pos2, pos3, pos4, pos5, pos6, w1, gain, w4_words, w4_scales, out
):
    nc = tc.nc
    with ExitStack() as ctx:
        lists = ctx.enter_context(tc.tile_pool(name="lists", bufs=1))
        keep = ctx.enter_context(tc.tile_pool(name="keep", bufs=1))
        ring = ctx.enter_context(tc.tile_pool(name="ring", bufs=4))
        pair = ctx.enter_context(tc.tile_pool(name="pair", bufs=2))
        split = ctx.enter_context(tc.tile_pool(name="split", bufs=1))
        sums = ctx.enter_context(tc.psum_pool(name="sums", bufs=4))
        turned = ctx.enter_context(tc.psum_pool(name="turned", bufs=4))

        def load_list(src, name):
            held = lists.tile(list(src.shape), U16, name=name)
            nc.sync.dma_start(held[:], src)
            return held

        def load_w1(a):
            raw = keep.tile([P, PACK, H], F32, name="w1_raw%d" % a)
            nc.sync.dma_start(raw[:], w1[a * P * PACK : (a + 1) * P * PACK, :].rearrange("(p j) r -> p j r", j=PACK))
            return raw

        def load_words(a):
            words = keep.tile([P, T], I32, name="table_words%d" % a)
            nc.sync.dma_start(words[:], tab_words[a].rearrange("p t i -> p (t i)").bitcast(I32))
            return words

        table_scales = keep.tile([P, T], U8, name="table_scales")
        nc.vector.memset(table_scales[:].bitcast(I32), 0)
        w4_plane = keep.tile([P, N], U8, name="w4_plane", align_bytes=64)
        nc.vector.memset(w4_plane[:].bitcast(I32), 0)

        idx = load_list(offs, "idx")
        for q in range(4):
            nc.sync.dma_start(
                table_scales[32 * q : 32 * q + 4 * PASSES, :].bitcast(I32),
                tab_scales[:, 4 * q : 4 * q + 4, :].bitcast(I32),
            )
        p2 = load_list(pos2, "p2")
        p1 = load_list(pos1, "p1")
        w1_raw, table_words = [], []
        for a in range(PASSES):
            w1_raw.append(load_w1(a))
            table_words.append(load_words(a))
        p3 = load_list(pos3, "p3")
        p4 = load_list(pos4, "p4")
        p5 = load_list(pos5, "p5")
        p6 = load_list(pos6, "p6")
        gains = keep.tile([P, PACK], F32, name="gains")
        nc.sync.dma_start(gains[:], gain.rearrange("(p t) -> p t", t=PACK))
        w4_codes = keep.tile([P, 2 * N], U8, name="w4_codes", align_bytes=64)
        nc.sync.dma_start(w4_codes[:].bitcast(I32), w4_words[0].bitcast(I32))
        for q in range(4):
            nc.sync.dma_start(
                w4_plane[32 * q : 32 * q + 4, :].bitcast(I32), w4_scales[0, 4 * q : 4 * q + 4, :].bitcast(I32)
            )

        identity = keep.tile([P, P], F32, name="identity")
        make_identity(nc, identity[:])
        minus_base = keep.tile([P, P], F32, name="minus_base")
        nc.gpsimd.memset(minus_base[:], -TURN_BASE)
        warm = keep.tile([P, 1], F32, name="warm")
        nc.scalar.activation(warm[:], identity[:, :1], ACT.Sin)

        picked_scales = keep.tile([P, S], U8, name="picked_scales", align_bytes=64)
        nc.vector.tensor_copy(picked_scales[:], table_scales[:].indirect(idx[:]))

        w1_codes, w1_planes, picked_words = [], [], []
        for a, (interleave, width) in enumerate(((nc.vector.tensor_copy, S), (nc.scalar.copy, CHUNK))):
            grouped = keep.tile([P, H * PACK], BF16, name="w1_grouped", tag="staged%d" % a, align_bytes=64)
            interleave(
                grouped[:].rearrange("p (t m j) -> p m j t", t=PACK, j=PACK),
                w1_raw[a][:].rearrange("p j (m t) -> p m j t", t=PACK),
            )
            w1_codes.append(keep.tile([P, H], U32, name="w1_codes%d" % a, align_bytes=64))
            w1_planes.append(keep.tile([P, H], U8, name="w1_plane%d" % a, align_bytes=64))
            nc.vector.quantize_mx(out=w1_codes[a][:].bitcast(FP8X4), scales=w1_planes[a][:], in_=grouped[:])
            picked_words.append(keep.tile([P, S], U32, name="picked_words", tag="staged%d" % a, align_bytes=64))
            for start in range(0, S, width):
                nc.vector.tensor_copy(
                    picked_words[a][:, start : start + width],
                    table_words[a][:].bitcast(U32).indirect(idx[:, start // LIST_ROWS : (start + width) // LIST_ROWS]),
                )

        h = [keep.tile([P, S], F32, name="h%d" % t) for t in range(PACK)]
        a3 = keep.tile([P, PACK, P3], F32, name="a3")

        to_bits = -BITS_PER_TURN / (2.0 * math.pi)
        to_turns = 1.0 / (2.0 * math.pi)

        def features_by_transposes(t, c0):
            rows = slice(t * P, (t + 1) * P)
            banks = []
            for c in (c0, c0 + 1):
                x = sums.tile([P, CHUNK], F32, name="x", tag="sums")
                for b in range(BLOCKS):
                    picks = slice(c * CHUNK + b * P, c * CHUNK + (b + 1) * P)
                    for a in range(PASSES):
                        nc.tensor.matmul_mx(
                            out=x[:, b * P : (b + 1) * P],
                            lhsT=picked_words[a][:, picks].bitcast(FP8X4),
                            lhsT_scale=picked_scales[4 * a :, picks],
                            rhs=w1_codes[a][:, rows].bitcast(FP8X4),
                            rhs_scale=w1_planes[a][:, rows],
                            start=(a == 0),
                            stop=(a == PASSES - 1),
                        )
                banks.append(x)
            parts = split.tile([P, 4 * CHUNK], U32, name="parts", tag="split%d" % (c0 // 2))
            whole = [parts[:, i * CHUNK : (i + 1) * CHUNK] for i in range(2)]
            turns = [parts[:, (2 + i) * CHUNK : (3 + i) * CHUNK].bitcast(F32) for i in range(2)]
            for i in (0, 1):
                nc.scalar.activation(whole[i], banks[i][:], ACT.Copy, scale=to_bits, bias=TURN_BASE_BITS)
            for i in (1, 0):
                nc.scalar.activation(turns[i], banks[i][:], ACT.Copy, scale=to_turns)
            for i in (1, 0):
                rest = turned.tile([P, CHUNK], F32, name="rest")
                for b in range(BLOCKS):
                    blk = slice(b * P, (b + 1) * P)
                    terms = (minus_base[:], whole[i][:, blk].bitcast(F32), turns[i][:, blk])
                    for n, term in enumerate(terms):
                        nc.tensor.matmul(
                            rest[:, blk], term, identity[:], is_transpose=True, start=(n == 0), stop=(n == 2)
                        )
                picks = slice((c0 + i) * CHUNK, (c0 + i + 1) * CHUNK)
                nc.scalar.activation(h[t][:, picks], rest[:], ACT.Sin, scale=2.0 * math.pi)

        def first_features():
            early = (CHUNKS - 1) * CHUNK
            rest_early = split.tile([P, early], F32, name="rest_early", tag="split0")
            rest_last = split.tile([P, CHUNK], F32, name="rest_last", tag="split1")
            for c in range(CHUNKS):
                last = c == CHUNKS - 1
                x = sums.tile([P, CHUNK], F32, name="x", tag="sums")
                picks = slice(c * CHUNK, (c + 1) * CHUNK)
                for a in range(PASSES):
                    nc.tensor.matmul_mx(
                        out=x[:],
                        lhsT=w1_codes[a][:, :P].bitcast(FP8X4),
                        lhsT_scale=w1_planes[a][:, :P],
                        rhs=picked_words[a][:, picks].bitcast(FP8X4),
                        rhs_scale=picked_scales[4 * a :, picks],
                        start=(a == 0),
                        stop=(a == PASSES - 1),
                    )
                turns = ring.tile([P, CHUNK], F32, name="turns")
                nc.scalar.activation(turns[:], x[:], ACT.Copy, scale=to_turns)
                whole = ring.tile([P, CHUNK], U32, name="whole")
                if last:
                    nc.vector.tensor_scalar(whole[:].bitcast(I32), x[:], to_bits, TURN_BASE_BITS, ALU.mult, ALU.add)
                else:
                    nc.scalar.activation(whole[:], x[:], ACT.Copy, scale=to_bits, bias=TURN_BASE_BITS)
                rest = rest_last[:] if last else rest_early[:, picks]
                nc.vector.scalar_tensor_tensor(
                    rest, whole[:].bitcast(F32), TURN_BASE, turns[:], ALU.subtract, ALU.add
                )
                if c == CHUNKS - 2:
                    nc.scalar.activation(h[0][:, :early], rest_early[:], ACT.Sin, scale=2.0 * math.pi)
            nc.scalar.activation(h[0][:, early:], rest_last[:], ACT.Sin, scale=2.0 * math.pi)

        def picks_of(held, start, width):
            return held[:, start // LIST_ROWS : (start + width) // LIST_ROWS]

        a2 = []

        def last_level_first_term(t, pieces):
            term = pair.tile([P, P3], F32, name="term", tag="right0", bufs=1)
            width = P3 // pieces
            for start in range(0, P3, width):
                nc.vector.tensor_copy(term[:, start : start + width], a2[t][:].indirect(picks_of(p5, start, width)))
            return term

        def last_level_sum(t, term, pieces):
            width = P3 // pieces
            for start in range(0, P3, width):
                own = slice(start, start + width)
                nc.vector.tensor_tensor(
                    a3[:, t, own], a2[t][:].indirect(picks_of(p6, start, width)), term[:, own], ALU.add
                )

        def levels(t):
            half = P1 // 2
            right = [pair.tile([P, half], F32, name="right", tag="right%d" % s, bufs=1) for s in range(2)]
            for s in range(2):
                nc.vector.tensor_scalar(
                    right[s][:], h[t][:].indirect(picks_of(p2, s * half, half)), 1.0, 1.0, ALU.mult, ALU.add
                )
            a1 = pair.tile([P, P1], F32, name="a1")
            for s in range(2):
                nc.vector.tensor_tensor(
                    a1[:, s * half : (s + 1) * half],
                    h[t][:].indirect(picks_of(p1, s * half, half)),
                    right[s][:],
                    ALU.mult,
                )
            term = last_level_first_term(t - 1, 1) if t else None
            first = pair.tile([P, P2], F32, name="first")
            second = pair.tile([P, P2], F32, name="second")
            nc.vector.tensor_copy(first[:], a1[:].indirect(p3[:]))
            nc.vector.tensor_copy(second[:], a1[:].indirect(p4[:]))
            if t:
                last_level_sum(t - 1, term, 1)
            a2.append(pair.tile([P, P2], F32, name="a2"))
            nc.vector.tensor_tensor(a2[t][:], first[:], second[:], ALU.min)

        first_features()
        levels(0)
        for t in range(1, PACK):
            for c0 in range(0, CHUNKS, 2):
                features_by_transposes(t, c0)
            levels(t)
        last_level_sum(PACK - 1, last_level_first_term(PACK - 1, HALVES), HALVES)

        halves = [slice(i * P3 // HALVES, (i + 1) * P3 // HALVES) for i in range(HALVES)]
        scaled = split.tile([P, PACK, P3], F32, name="scaled", tag="split1")
        for t in range(PACK - 1):
            nc.scalar.activation(scaled[:, t, :], a3[:, t, :], ACT.Copy, scale=gains[:, t : t + 1])
        for own in halves:
            nc.vector.tensor_scalar_mul(scaled[:, PACK - 1, own], a3[:, PACK - 1, own], gains[:, PACK - 1 :])
        a3_grouped = keep.tile([P, P3, PACK], BF16, name="a3_grouped", align_bytes=64)
        for own in halves:
            nc.vector.tensor_copy(
                a3_grouped[:, own, :].rearrange("p (c i) t -> p c t i", i=PACK),
                scaled[:, :, own].rearrange("p t (c i) -> p c t i", i=PACK),
            )
        a3_codes = keep.tile([P, P3], U32, name="a3_codes", align_bytes=64)
        a3_plane = keep.tile([P, P3], U8, name="a3_plane", align_bytes=64)
        for own in halves:
            nc.vector.quantize_mx(
                out=a3_codes[:, own].bitcast(FP8X4),
                scales=a3_plane[:, own],
                in_=a3_grouped[:, own, :].rearrange("p j t -> p (j t)"),
            )

        for b in range(N // P):
            y = sums.tile([P, P3], F32, name="y", tag="sums")
            nc.tensor.matmul_mx(
                out=y[:],
                lhsT=w4_codes[:, 2 * P * b : 2 * P * (b + 1)].bitcast(FP4X4),
                lhsT_scale=w4_plane[:, P * b : P * (b + 1)],
                rhs=a3_codes[:].bitcast(FP8X4),
                rhs_scale=a3_plane[:],
                start=True,
                stop=True,
            )
            scores = ring.tile([P, P3], F32, name="scores")
            nc.scalar.activation(scores[:], y[:], ACT.Sigmoid)
            nc.sync.dma_start(out[P * b : P * (b + 1), :], scores[:])
